import numpy as np, ml_dtypes
CORES = [0,1,2,3,4,5,6,7]
N = 8
def setup_inputs(rng):
    return {"x": rng.standard_normal((N, 128, 256), dtype=np.float32).astype(ml_dtypes.bfloat16)}
def reference(x):
    g = np.concatenate(list(x), axis=1)
    return {"y": np.broadcast_to(g, (N,) + g.shape)}

from concourse.bass import DstId, RemoteDMATransfer

W = 256
N = 8

SCRATCH = {
    "land": ("sbuf", [128, N * W], "bfloat16"),
}
SEMAPHORES = ["loaded", "read", "arrived", "stored"]

ENGINES = 16


def rank_program(g, core, T, topo):
    rank = T.rank_of(core)
    if rank is None:
        return
    peers = [c for c in T.cores if c != core]
    blk = T.land[:, rank * W:(rank + 1) * W]

    g.dma_start(blk, T.x[:]).then_inc(T.sem.loaded, 16)
    g.wait_ge(T.sem.loaded, 16)

    g.remote_dma_fused(
        [RemoteDMATransfer(
            dst_ids=[DstId(rid=topo.addr(p)[0], pnc=topo.addr(p)[1]) for p in peers],
            dma_engine_mask=topo.mask(core, peers[0]),
            remote_sem=T.sem.arrived,
            srcs=[blk],
            dsts=[blk for p in peers],
        )],
        local_sem=T.sem.read,
    )

    g.wait_ge(T.sem.arrived, ENGINES * len(peers))
    g.wait_ge(T.sem.read, ENGINES)
    g.dma_start(T.y[:], T.land[:]).then_inc(T.sem.stored, 16)
    g.wait_ge(T.sem.stored, 16)
